import numpy as np
import ml_dtypes


def mxq(x, axis, fmt="e4m3"):
    dtype, down = {"e4m3": (ml_dtypes.float8_e4m3fn, 7), "e5m2": (ml_dtypes.float8_e5m2, 14)}[fmt]
    v = np.moveaxis(np.asarray(x, np.float32).astype(ml_dtypes.bfloat16).astype(np.float64), axis, -1)
    blocks = v.reshape(v.shape[:-1] + (-1, 32))
    amax = np.abs(blocks).max(-1, keepdims=True)
    byte = np.maximum(np.where(amax > 0, np.frexp(amax)[1] - 1 + 127, 0) - down, 1)
    scale = np.exp2(byte - 127.0)
    codes = (blocks / scale).astype(np.float32).astype(dtype).astype(np.float64)
    return np.moveaxis((codes * scale).reshape(v.shape), -1, axis)


WIDE = False


def mx_kscale(k):
    if not WIDE:
        return np.ones(k)
    levels = np.array([10, -10, 5, -5, 0])
    if k % 512:
        return np.exp2(np.random.permutation(np.resize(levels, k // 32))).repeat(32)
    a = np.empty((k // 512, 16))
    for p in range(k // 512):
        a[p, :8] = np.random.permutation(np.resize(levels, 8))
        for g in range(8):
            far = levels[np.abs(levels - a[p, g]) >= 10]
            a[p, g + 8] = far[np.random.randint(len(far))]
    return np.exp2(a.ravel()).repeat(32)


BF16 = ml_dtypes.bfloat16


def bf(x):
    return np.asarray(x, np.float32).astype(BF16)


def f64(x):
    return np.asarray(x).astype(np.float64)


N, T, D, A = 384, 4, 1024, 1024


def adapter_scores(q, k):
    d = q.shape[-1]
    return np.sum(q[None, :, :] * k, axis=-1) / np.sqrt(d)


def softmax0(s):
    e = np.exp(s - s.max(axis=0, keepdims=True))
    return e / e.sum(axis=0, keepdims=True)


def draw0():
    u, v = mx_kscale(D), mx_kscale(D)
    return {
        "x": bf(np.random.standard_normal((N, D))),
        "z": bf(np.random.standard_normal((T, N, D)) * u),
        "wq": bf(np.random.standard_normal((D, A)) / np.sqrt(D)),
        "wk": bf(np.random.standard_normal((D, A)) / np.sqrt(D) / u[:, None]),
        "wv": bf(np.random.standard_normal((D, D)) / np.sqrt(D) / v[:, None]),
        "g": bf((1.0 + 0.1 * np.random.standard_normal(D)) * v / u),
    }


def core(x, z, wq, wk, wv, g):
    x, z, g = f64(x), f64(z), f64(g)
    q = x @ f64(wq)
    k = mxq(z, 2, "e4m3") @ mxq(f64(wk), 0, "e4m3")
    s = adapter_scores(q, k)
    p = softmax0(s)
    mix = np.sum(p[:, :, None] * z, axis=0)
    c = g[None, :] * mix
    return x + (mxq(c, 1, "e4m3") @ mxq(f64(wv), 0, "e4m3"))


def e4m3fn_bytes(y):
    return np.clip(np.asarray(y, np.float64), -448.0, 448.0).astype(np.float32).astype(ml_dtypes.float8_e4m3fn).view(np.uint8)


def e4m3fn_values(b):
    return np.asarray(b, np.uint8).view(ml_dtypes.float8_e4m3fn).astype(np.float64)


def setup_inputs():
    d = draw0()
    x0 = np.asarray(d['wv']).astype(np.float64)
    s = (np.max(np.abs(x0), axis=(1,), keepdims=True) / 448.0).astype(np.float32)
    out = {}
    for k, v in d.items():
        if k == 'wv':
            out['wv_bytes'] = e4m3fn_bytes(x0 / s.astype(np.float64))
            out['wv_scale'] = s
        else:
            out[k] = v
    return out


def reference(x, z, wq, wk, wv_bytes, wv_scale, g):
    return core(x, z, wq, wk, e4m3fn_values(wv_bytes) * wv_scale.astype(np.float64), g)

@@ -1,0 +1,344 @@
+from contextlib import ExitStack
+
+import concourse.mybir as mybir
+from concourse.masks import make_identity
+
+N, T, D, A = 384, 4, 1024, 1024
+FLOPS = 2 * N * D * A + 2 * T * N * D * A + 2 * N * D * D
+
+F32 = mybir.dt.float32
+BF16 = mybir.dt.bfloat16
+U32 = mybir.dt.uint32
+U8 = mybir.dt.uint8
+FP8 = mybir.dt.float8_e4m3fn
+FP8X4 = mybir.dt.float8_e4m3fn_x4
+ALU = mybir.AluOpType
+ACT = mybir.ActivationFunctionType
+AX = mybir.AxisListType
+
+P = 128
+PASSES = 2
+HALF = 512
+TILES = N // P
+WK_SCALAR = (176, 256)
+MODES = ('S2', 'S2', 'D')
+LAST = {"D": (0, 1, 2, 3), "S2": (1, 3), "C": (1, 3), "A": (3,)}
+WV_ENGINE = 'SSGGSSGG'
+D_SCALAR = (0, 1)
+PART_BUFS = {'pr0': 3, 'ch1': 3, 'pr2': 3, 'ch3': 3, 'pr3': 2, 'pr1': 2}
+TP_BANKS, ACC_BANKS = 3, 5
+LOADS = "x1 z02 x2 x0 wqA0 z01 wqA1 z21 wkA0 wkA1 z13 z00 z10 z03 z12 wqB0 wkB1 wqB1 wkB0 z20 z22 z11 wv1 wv0 z23"
+ORDER = (
+    "wkiVA0 xT1 xT0 xTc1 xT2 xTc0 zT02 q1A0 xTc2 q2A0 q0A0 q1A1 "
+    "wkiSA0 zTc02 q0A1 qc1A q2A1 zT00 wkiSA1 wkiVA1 zT10 zq02 zT03 zTc00 "
+    "wkqA1 zT01 zTc10 wkqA0 zTc03 zTc01 zT12 zq00 zT21 zq01 qc2A zT13 "
+    "zTc21 zq21 zq03 k01A qc0A k00A wkiVB1 wkiSB1 zTc12 zq10 sc00A k02A "
+    "zTc13 q0B0 q0B1 wkiVB0 zT20 zT22 wkiSB0 qc0B wkqB1 sc01A zTc22 zTc20 "
+    "zT11 wkqB0 k03A zTc11 sc02A zq12 k00B zq13 wd11 sc03A wd00 k02B "
+    "k01B sc00B zq11 wd03 sc02B k12A k03B q1B0 q1B1 zq20 k13B sc12A "
+    "sc03B wd13 sc01B qc1B wd02 sadd0 zq22 smax0 k10B k22A wd10 sc13B "
+    "k12B sc10B exp0 k13A sc22A wd01 sc12B k10A k11B rec0 sc13A p0 "
+    "pr000 sc10A zT23 sc11B pr010 k11A wvi03 sc11A q2B0 ch001 sadd1 ch011 "
+    "pr012 zTc23 pr002 q2B1 smax1 zq23 ch003 k21A ch013 qc2B k20A sc21A "
+    "wd12 k22B k21B exp1 sc22B k23A sc20A rec1 cT00 wvi12 sc21B p1 "
+    "sc23A k23B wvi11 sc23B wvi01 pr110 k20B wvi13 pr112 pr102 cT01 sc20B "
+    "cg01 sadd2 pr100 ch113 smax2 exp2 wvi00 ch101 rec2 ch103 p2 pr210 "
+    "ch111 cT10 wvi10 cg00 pr202 cg10 cT11 pr203 pr200 pr201 wvi02 cT20 "
+    "pr212 pr213 cg11 wvq1 wvq0 cq0 pr211 cg20 cT21 cv0A cq1 cg21 "
+    "cv0B fin0A cq2 cv1A cv1B fin1A cv2B fin1B fin0B cv2A fin2A fin2B "
+)
+
+
+def tile_adapterfusiontokenmixture_kernel(tc, x, z, wq, wk, wv_bytes, wv_scale, g, out):
+    nc = tc.nc
+    with ExitStack() as ctx:
+        keep = ctx.enter_context(tc.tile_pool(name="keep", bufs=1))
+        work = ctx.enter_context(tc.tile_pool(name="work", bufs=2))
+        psum = ctx.enter_context(tc.psum_pool(name="psum", bufs=1))
+
+        ident = keep.tile([P, P], F32, name="ident")
+        make_identity(nc, ident[:])
+        warm = keep.tile([P, 2], F32, name="warm")
+        nc.vector.memset(warm[:], 0.0)
+        nc.scalar.activation(out=warm[:, 1:2], in_=warm[:, 0:1], func=ACT.Exp)
+
+        x_sb = [keep.tile([P, D], BF16, name=f"x{i}") for i in range(TILES)]
+        z_sb = [[keep.tile([P, D], BF16, name=f"z{i}_{t}") for t in range(T)] for i in range(TILES)]
+        wq_sb = [keep.tile([P, 4, 2, HALF], BF16, name=f"wq{h}") for h in range(2)]
+        wk_sb = [[keep.tile([P, 4, HALF], BF16, name=f"wk{h}_{c}") for c in range(PASSES)] for h in range(2)]
+        wv_sb = [keep.tile([P, 4, D], U8, name=f"wvb{c}") for c in range(PASSES)]
+        wvs_sb = keep.tile([P, PASSES, 4], F32, name="wvs")
+        g_sb = keep.tile([P, PASSES, 4], BF16, name="gsb")
+
+        wq_v = wq.rearrange("(b p e) a -> b p e a", p=P, e=2)
+        wk_v = wk.rearrange("(c p j) a -> c p j a", p=P, j=4)
+        wv_v = wv_bytes.rearrange("(c p j) n -> c p j n", p=P, j=4)
+
+        def load(name):
+            h = 1 if "B" in name else 0
+            cols = slice(h * HALF, (h + 1) * HALF)
+            k = int(name[-1])
+            if name.startswith("x"):
+                nc.sync.dma_start(out=x_sb[k][:], in_=x[k * P : (k + 1) * P, :])
+            elif name.startswith("z"):
+                i = int(name[1])
+                nc.sync.dma_start(out=z_sb[i][k][:], in_=z[k, i * P : (i + 1) * P, :])
+            elif name.startswith("wq"):
+                for b in (2 * k, 2 * k + 1):
+                    nc.sync.dma_start(out=wq_sb[h][:, b, :, :], in_=wq_v[b, :, :, cols])
+            elif name.startswith("wk"):
+                nc.sync.dma_start(out=wk_sb[h][k][:], in_=wk_v[k, :, :, cols])
+            else:
+                nc.sync.dma_start(out=wv_sb[k][:], in_=wv_v[k])
+
+        nc.gpsimd.dma_start(out=wvs_sb[:], in_=wv_scale.rearrange("(c p j) o -> p c (j o)", p=P, j=4))
+        nc.gpsimd.dma_start(out=g_sb[:], in_=g.rearrange("(c p j) -> p c j", p=P, j=4))
+        for name in LOADS.split():
+            load(name)
+
+        wk_codes = [keep.tile([P, PASSES, HALF], U32, align_bytes=64, name=f"wkc{h}") for h in range(2)]
+        wk_scales = [keep.tile([P, PASSES, HALF], U8, align_bytes=64, name=f"wks{h}") for h in range(2)]
+        wv_codes = [keep.tile([P, D], U32, align_bytes=64, name=f"wvc{c}") for c in range(PASSES)]
+        wv_scales = [keep.tile([P, D], U8, align_bytes=64, name=f"wvx{c}") for c in range(PASSES)]
+        xT_sb = [keep.tile([P, 4, P], F32, name=f"xT{i}") for i in range(TILES)]
+        q_sb = [keep.tile([P, A], F32, name=f"q{i}") for i in range(TILES)]
+        zq_codes = [[keep.tile([P, PASSES, P], U32, align_bytes=64, name=f"zc{i}_{t}") for t in range(T)] for i in range(TILES)]
+        zq_scales = [[keep.tile([P, PASSES, P], U8, align_bytes=64, name=f"zs{i}_{t}") for t in range(T)] for i in range(TILES)]
+        s_parts = [keep.tile([P, T, 2], F32, name=f"sp{i}") for i in range(TILES)]
+        p_sb = [keep.tile([P, T], F32, name=f"p{i}") for i in range(TILES)]
+        c_codes = [keep.tile([P, PASSES, P], U32, align_bytes=64, name=f"cc{i}") for i in range(TILES)]
+        c_scales = [keep.tile([P, PASSES, P], U8, align_bytes=64, name=f"cs{i}") for i in range(TILES)]
+
+        def tp_bank():
+            bank = psum.tile([P, 4, P], F32, name="tp", tag="tp", bufs=TP_BANKS)
+            return bank
+
+        def acc_bank():
+            bank = psum.tile([P, HALF], F32, name="acc", tag="acc", bufs=ACC_BANKS)
+            return bank
+
+
+        wk_mid, banks, z_mid, neg, low, e_sb, total, parts, c_mid, wv_wide, wv_mid = ({} for _ in range(11))
+
+        def wk_tile(h, c):
+            if (h, c) not in wk_mid:
+                mid = work.tile([P, HALF, 4], BF16, align_bytes=64, name="wkmid", bufs=4)
+                wk_mid[h, c] = mid
+            return wk_mid[h, c]
+
+        def cols_of(h):
+            return slice(h * HALF, (h + 1) * HALF)
+
+        def do(op):
+            kind = "".join(ch for ch in op if ch not in "0123456789AB")
+            rest = op[len(kind):]
+            if kind in ("wkiS", "wkiV", "wkq"):
+                h, c = "AB".index(rest[0]), int(rest[1])
+                mid = wk_tile(h, c)
+                src = wk_sb[h][c][:].rearrange("p j n -> p n j")
+                w = WK_SCALAR[h]
+                if kind == "wkiS":
+                    nc.scalar.copy(out=mid[:, :w, :], in_=src[:, :w, :])
+                elif kind == "wkiV":
+                    nc.vector.tensor_copy(out=mid[:, w:, :], in_=src[:, w:, :])
+                else:
+                    nc.vector.quantize_mx(
+                        out=wk_codes[h][:, c, :].bitcast(FP8X4),
+                        scales=wk_scales[h][:, c, :],
+                        in_=mid[:].rearrange("p n j -> p (n j)"),
+                    )
+                return
+            if kind in ("wd", "wvi", "wvq"):
+                c = int(rest[0])
+                if kind == "wd":
+                    j = int(rest[1])
+                    if c not in wv_wide:
+                        wide = keep.tile([P, 4, D], BF16, name=f"wvw{c}")
+                        wv_wide[c] = wide
+                    nc.scalar.activation(
+                        out=wv_wide[c][:, j, :], in_=wv_sb[c][:, j, :].bitcast(FP8), func=ACT.Copy, scale=wvs_sb[:, c, j : j + 1]
+                    )
+                elif kind == "wvi":
+                    s = int(rest[1])
+                    if c not in wv_mid:
+                        mid = keep.tile([P, D, 4], BF16, align_bytes=64, name=f"wvm{c}")
+                        wv_mid[c] = mid
+                    cols = slice(256 * s, 256 * (s + 1))
+                    src = wv_wide[c][:, :, cols].rearrange("p j n -> p n j")
+                    dst = wv_mid[c][:, cols, :]
+                    eng = WV_ENGINE[4 * c + s]
+                    if eng == "S":
+                        nc.scalar.copy(out=dst, in_=src)
+                    elif eng == "V":
+                        nc.vector.tensor_copy(out=dst, in_=src)
+                    else:
+                        nc.gpsimd.tensor_scalar(out=dst, in0=src, scalar1=1.0, scalar2=0.0, op0=ALU.mult, op1=ALU.add)
+                else:
+                    nc.vector.quantize_mx(
+                        out=wv_codes[c][:].bitcast(FP8X4), scales=wv_scales[c][:], in_=wv_mid[c][:].rearrange("p n j -> p (n j)")
+                    )
+                return
+            i = int(rest[0])
+            if kind == "xT":
+                bank = tp_bank()
+                banks["x", i] = bank
+                words = x_sb[i][:].bitcast(F32)
+                for b in range(4):
+                    nc.tensor.transpose(bank[:, b, :], words[:, b * P : (b + 1) * P], ident[:])
+            elif kind == "xTc":
+                nc.scalar.copy(out=xT_sb[i][:], in_=banks["x", i][:])
+            elif kind == "q":
+                h, part = "AB".index(rest[1]), int(rest[2])
+                if part == 0:
+                    acc = acc_bank()
+                    banks["q", i, h] = acc
+                xT = xT_sb[i][:].rearrange("p b n -> p (b n)").bitcast(BF16)
+                for b in (2 * part, 2 * part + 1):
+                    for e in range(2):
+                        nc.tensor.matmul(
+                            out=banks["q", i, h][:],
+                            lhsT=xT[:, 2 * b * P + e : 2 * (b + 1) * P : 2],
+                            rhs=wq_sb[h][:, b, e, :],
+                            start=(b == 0 and e == 0),
+                            stop=(b == 3 and e == 1),
+                        )
+            elif kind == "qc":
+                h = "AB".index(rest[1])
+                nc.scalar.copy(out=q_sb[i][:, cols_of(h)], in_=banks["q", i, h][:])
+            elif kind == "zT":
+                t = int(rest[1])
+                bank = tp_bank()
+                banks["z", i, t] = bank
+                words = z_sb[i][t][:].bitcast(F32)
+                for c in range(PASSES):
+                    for u in range(2):
+                        nc.tensor.transpose(bank[:, 2 * c + u, :], words[:, 256 * c + u : 256 * (c + 1) : 2], ident[:])
+            elif kind == "zTc":
+                t = int(rest[1])
+                mid = work.tile([P, PASSES, P, 2], F32, align_bytes=64, name="zmid", bufs=6)
+                z_mid[i, t] = mid
+                nc.scalar.copy(out=mid[:], in_=banks["z", i, t][:].rearrange("p (c u) n -> p c n u", u=2))
+            elif kind == "zq":
+                t = int(rest[1])
+                nc.vector.quantize_mx(
+                    out=zq_codes[i][t][:].rearrange("p c n -> p (c n)").bitcast(FP8X4),
+                    scales=zq_scales[i][t][:].rearrange("p c n -> p (c n)"),
+                    in_=z_mid[i, t][:].rearrange("p c n u -> p (c n u)").bitcast(BF16),
+                )
+            elif kind == "k":
+                t, h = int(rest[1]), "AB".index(rest[2])
+                acc = acc_bank()
+                banks["k", i, t, h] = acc
+                for c in range(PASSES):
+                    nc.tensor.matmul_mx(
+                        out=acc[:],
+                        lhsT=zq_codes[i][t][:, c, :].bitcast(FP8X4),
+                        lhsT_scale=zq_scales[i][t][:, c, :],
+                        rhs=wk_codes[h][:, c, :].bitcast(FP8X4),
+                        rhs_scale=wk_scales[h][:, c, :],
+                        start=(c == 0),
+                        stop=(c == PASSES - 1),
+                    )
+            elif kind == "sc":
+                t, h = int(rest[1]), "AB".index(rest[2])
+                junk = work.tile([P, HALF], F32, name="junk", bufs=2)
+                nc.vector.scalar_tensor_tensor(
+                    out=junk[:],
+                    in0=banks["k", i, t, h][:],
+                    scalar=-1.0 / 32.0,
+                    in1=q_sb[i][:, cols_of(h)],
+                    op0=ALU.mult,
+                    op1=ALU.mult,
+                    accum_out=s_parts[i][:, t, h : h + 1],
+                )
+            elif kind == "sadd":
+                tile = work.tile([P, T], F32, name="neg", bufs=3)
+                neg[i] = tile
+                nc.vector.tensor_reduce(out=tile[:], in_=s_parts[i][:], axis=AX.X, op=ALU.add)
+            elif kind == "smax":
+                tile = work.tile([P, 1], F32, name="low", bufs=3)
+                low[i] = tile
+                nc.vector.tensor_reduce(out=tile[:], in_=neg[i][:], axis=AX.X, op=ALU.min)
+            elif kind == "exp":
+                e = work.tile([P, T], F32, name="e", bufs=3)
+                s = work.tile([P, 1], F32, name="total", bufs=3)
+                e_sb[i], total[i] = e, s
+                nc.scalar.activation(out=e[:], in_=neg[i][:], func=ACT.Exp, bias=low[i][:], scale=-1.0, accum_out=s[:])
+            elif kind == "rec":
+                inv = work.tile([P, 1], F32, name="inv", bufs=3)
+                total[i, "inv"] = inv
+                nc.vector.reciprocal(out=inv[:], in_=total[i][:])
+            elif kind == "p":
+                nc.vector.tensor_scalar(out=p_sb[i][:], in0=e_sb[i][:], scalar1=total[i, "inv"][:], scalar2=None, op0=ALU.mult)
+            elif kind in ("pr", "ch"):
+                c, t = int(rest[1]), int(rest[2])
+                src = z_sb[i][t][:, 512 * c : 512 * (c + 1)].rearrange("p (n j) -> p j n", j=4)
+                part = work.tile([P, 4, P], F32, name=f"{kind}{t}", bufs=PART_BUFS[kind + str(t)])
+                weight = p_sb[i][:, t : t + 1]
+                if kind == "ch":
+                    prev = parts[i, c, t - 1]
+                    nc.vector.scalar_tensor_tensor(
+                        out=part[:], in0=src, scalar=weight, in1=prev[:], op0=ALU.mult, op1=ALU.add
+                    )
+                elif (MODES[i] == "D" and t in D_SCALAR) or MODES[i] in ("S2", "A") or (MODES[i] == "C" and t == 0):
+                    nc.scalar.activation(out=part[:], in_=src, func=ACT.Copy, scale=weight)
+                else:
+                    nc.vector.tensor_scalar(out=part[:], in0=src, scalar1=weight, scalar2=None, op0=ALU.mult)
+                parts[i, c, t] = part
+            elif kind == "cT":
+                c = int(rest[1])
+                bank = tp_bank()
+                banks["c", i, c] = bank
+                tiles = [parts[i, c, t] for t in LAST[MODES[i]]]
+                for j in range(4):
+                    for n in range(len(tiles)):
+                        nc.tensor.matmul(
+                            out=bank[:, j, :],
+                            lhsT=tiles[n][:, j, :],
+                            rhs=ident[:],
+                            is_transpose=True,
+                            start=(n == 0),
+                            stop=(n == len(tiles) - 1),
+                        )
+            elif kind == "cg":
+                c = int(rest[1])
+                if i not in c_mid:
+                    mid = work.tile([P, PASSES, P, 4], BF16, align_bytes=64, name="cmid", bufs=3)
+                    c_mid[i] = mid
+                nc.vector.tensor_tensor(
+                    out=c_mid[i][:, c, :, :],
+                    in0=banks["c", i, c][:].rearrange("p j n -> p n j"),
+                    in1=g_sb[:, c, :].unsqueeze(1).to_broadcast([P, P, 4]),
+                    op=ALU.mult,
+                )
+            elif kind == "cq":
+                nc.vector.quantize_mx(
+                    out=c_codes[i][:].rearrange("p c n -> p (c n)").bitcast(FP8X4),
+                    scales=c_scales[i][:].rearrange("p c n -> p (c n)"),
+                    in_=c_mid[i][:].rearrange("p c n j -> p (c n j)"),
+                )
+            elif kind == "cv":
+                h = "AB".index(rest[1])
+                acc = acc_bank()
+                banks["o", i, h] = acc
+                for c in range(PASSES):
+                    nc.tensor.matmul_mx(
+                        out=acc[:],
+                        lhsT=c_codes[i][:, c, :].bitcast(FP8X4),
+                        lhsT_scale=c_scales[i][:, c, :],
+                        rhs=wv_codes[c][:, cols_of(h)].bitcast(FP8X4),
+                        rhs_scale=wv_scales[c][:, cols_of(h)],
+                        start=(c == 0),
+                        stop=(c == PASSES - 1),
+                    )
+            elif kind == "fin":
+                h = "AB".index(rest[1])
+                res = work.tile([P, HALF], F32, name="res", bufs=3)
+                nc.vector.tensor_tensor(out=res[:], in0=banks["o", i, h][:], in1=x_sb[i][:, cols_of(h)], op=ALU.add)
+                nc.sync.dma_start(out=out[i * P : (i + 1) * P, cols_of(h)], in_=res[:])
+            else:
+                raise ValueError(op)
+
+        with tc.manual_schedule():
+            for op in ORDER.split():
+                do(op)

@@ -20,32 +20,35 @@ P = 128
 PASSES = 2
 HALF = 512
 TILES = N // P
-WK_SCALAR = (176, 256)
-MODES = ('S2', 'S2', 'D')
-LAST = {"D": (0, 1, 2, 3), "S2": (1, 3), "C": (1, 3), "A": (3,)}
-WV_ENGINE = 'SSGGSSGG'
-D_SCALAR = (0, 1)
-PART_BUFS = {'pr0': 3, 'ch1': 3, 'pr2': 3, 'ch3': 3, 'pr3': 2, 'pr1': 2}
+WK_SCALAR = (0, 0, 0, 512)
+WD_ENGINE = 'SSSSVSVV'
+ZP = '000000000000'
+WARM = 6
+MODES = ('D012', 'D012', 'D012')
+LAST = {"D0": (0, 1, 2, 3), "D01": (0, 1, 2, 3), "D012": (0, 1, 2, 3), "S2": (1, 3), "C": (1, 3), "A": (3,)}
+WV_ENGINE = 'VSSSVSVV'
+PART_BUFS = {'pr2': 4, 'pr3': 4, 'pr0': 3, 'pr1': 3}
 TP_BANKS, ACC_BANKS = 3, 5
-LOADS = "x1 z02 x2 x0 wqA0 z01 wqA1 z21 wkA0 wkA1 z13 z00 z10 z03 z12 wqB0 wkB1 wqB1 wkB0 z20 z22 z11 wv1 wv0 z23"
+LOADS = "z00 x0 x12 wq0 zz0 z03 wq1 wv1 wq2 wk1 wq3 wk0 z02 z01 zz3 zz2 zz1 wv0"
 ORDER = (
-    "wkiVA0 xT1 xT0 xTc1 xT2 xTc0 zT02 q1A0 xTc2 q2A0 q0A0 q1A1 "
-    "wkiSA0 zTc02 q0A1 qc1A q2A1 zT00 wkiSA1 wkiVA1 zT10 zq02 zT03 zTc00 "
-    "wkqA1 zT01 zTc10 wkqA0 zTc03 zTc01 zT12 zq00 zT21 zq01 qc2A zT13 "
-    "zTc21 zq21 zq03 k01A qc0A k00A wkiVB1 wkiSB1 zTc12 zq10 sc00A k02A "
-    "zTc13 q0B0 q0B1 wkiVB0 zT20 zT22 wkiSB0 qc0B wkqB1 sc01A zTc22 zTc20 "
-    "zT11 wkqB0 k03A zTc11 sc02A zq12 k00B zq13 wd11 sc03A wd00 k02B "
-    "k01B sc00B zq11 wd03 sc02B k12A k03B q1B0 q1B1 zq20 k13B sc12A "
-    "sc03B wd13 sc01B qc1B wd02 sadd0 zq22 smax0 k10B k22A wd10 sc13B "
-    "k12B sc10B exp0 k13A sc22A wd01 sc12B k10A k11B rec0 sc13A p0 "
-    "pr000 sc10A zT23 sc11B pr010 k11A wvi03 sc11A q2B0 ch001 sadd1 ch011 "
-    "pr012 zTc23 pr002 q2B1 smax1 zq23 ch003 k21A ch013 qc2B k20A sc21A "
-    "wd12 k22B k21B exp1 sc22B k23A sc20A rec1 cT00 wvi12 sc21B p1 "
-    "sc23A k23B wvi11 sc23B wvi01 pr110 k20B wvi13 pr112 pr102 cT01 sc20B "
-    "cg01 sadd2 pr100 ch113 smax2 exp2 wvi00 ch101 rec2 ch103 p2 pr210 "
-    "ch111 cT10 wvi10 cg00 pr202 cg10 cT11 pr203 pr200 pr201 wvi02 cT20 "
-    "pr212 pr213 cg11 wvq1 wvq0 cq0 pr211 cg20 cT21 cv0A cq1 cg21 "
-    "cv0B fin0A cq2 cv1A cv1B fin1A cv2B fin1B fin0B cv2A fin2A fin2B "
+    "xT0 zT00 xTc0 zTc00 xT2 xT1 q0A0 q0B0 xTc2 q2B0 xTc1 q1A0 "
+    "zT20 zT03 zT10 q2A0 q2B1 zTc03 wd13 zTc10 q0B1 zTc20 zq10 wd10 "
+    "q0A1 q1A1 wd12 q2A1 wd11 q0B2 q2B2 q2A2 q1A2 q0A2 wvi13 wvi10 "
+    "wkiSB1 wkiVA1 q0A3 qc0A q1A3 zq20 qc1A wvi12 zq00 wkqA1 q0B3 qc0B "
+    "q2B3 q2A3 zT01 zT02 wkiVB0 zT23 zTc01 zT13 wkiVA0 zTc02 wkqB0 qc2B "
+    "wkqA0 zT12 zTc23 wkqB1 zq02 zTc12 qc2A zq01 k00A zq03 zTc13 wd01 "
+    "k00B k01B k03A k02A wd00 zT11 zq12 sc00A zT22 sc00B k03B sc03A "
+    "zq23 sc02A wvi11 sc01B zTc11 k02B sc03B wd03 k01A zq13 sc02B zTc22 "
+    "sc01A q1B0 zq11 k12A sadd0 smax0 exp0 wd02 k13A q1B1 q1B2 sc13A "
+    "q1B3 rec0 k10A qc1B k10B zq22 p0 k13B sc12A k11A pr012 wvi03 "
+    "pr013 k12B sc10A sc10B sc13B sc11A k11B wvi01 pr002 k22A zT21 sc12B "
+    "zTc21 pr000 sc11B pr003 sadd1 k20B sc22A smax1 exp1 wvi02 zq21 sc20B "
+    "k23B k23A k21A k22B pr011 rec1 sc23A sc23B p1 pr010 pr101 sc22B "
+    "k20A pr112 k21B cT01 pr001 pr100 sc21A sc21B sc20A pr103 sadd2 pr102 "
+    "pr113 smax2 cT00 exp2 pr110 pr111 cg01 rec2 cg00 cT10 cT11 p2 "
+    "pr211 wvq1 cg10 pr213 pr212 wvi00 pr203 pr200 pr210 wvq0 cT21 pr201 "
+    "cq0 cg11 pr202 cg21 cT20 cg20 cq1 cq2 cv0A cv0B cv2B fin0B "
+    "cv1B fin0A fin2B cv1A cv2A fin1B fin1A fin2A "
 )
 
 
@@ -62,45 +65,64 @@ def tile_adapterfusiontokenmixture_kernel(tc, x, z, wq, wk, wv_bytes, wv_scale, 
         nc.vector.memset(warm[:], 0.0)
         nc.scalar.activation(out=warm[:, 1:2], in_=warm[:, 0:1], func=ACT.Exp)
 
-        x_sb = [keep.tile([P, D], BF16, name=f"x{i}") for i in range(TILES)]
-        z_sb = [[keep.tile([P, D], BF16, name=f"z{i}_{t}") for t in range(T)] for i in range(TILES)]
-        wq_sb = [keep.tile([P, 4, 2, HALF], BF16, name=f"wq{h}") for h in range(2)]
-        wk_sb = [[keep.tile([P, 4, HALF], BF16, name=f"wk{h}_{c}") for c in range(PASSES)] for h in range(2)]
+        x0 = keep.tile([P, D], BF16, name="x0")
+        x12 = keep.tile([P, 2, D], BF16, name="x12")
+        x_sb = [x0[:], x12[:, 0, :], x12[:, 1, :]]
+        z0 = [keep.tile([P, D], BF16, name=f"z0_{t}") for t in range(T)]
+        z12 = [keep.tile([P, 2, D], BF16, name=f"z12_{t}") for t in range(T)]
+        z_sb = [[z0[t][:] for t in range(T)], [z12[t][:, 0, :] for t in range(T)], [z12[t][:, 1, :] for t in range(T)]]
+        wq_sb = [keep.tile([P, 2, A], BF16, name=f"wq{b}") for b in range(4)]
+        wk_sb = [keep.tile([P, 4, A], BF16, name=f"wk{c}") for c in range(PASSES)]
         wv_sb = [keep.tile([P, 4, D], U8, name=f"wvb{c}") for c in range(PASSES)]
         wvs_sb = keep.tile([P, PASSES, 4], F32, name="wvs")
         g_sb = keep.tile([P, PASSES, 4], BF16, name="gsb")
 
+        if WARM:
+            zero = keep.tile([P, HALF], BF16, name="zero")
+            nc.vector.memset(zero[:], 0.0)
+            bank = psum.tile([P, HALF], F32, name="acc", tag="acc", bufs=5)
+            for n in range(WARM):
+                nc.tensor.matmul(out=bank[:], lhsT=zero[:, :P], rhs=zero[:], start=True, stop=True)
         wq_v = wq.rearrange("(b p e) a -> b p e a", p=P, e=2)
         wk_v = wk.rearrange("(c p j) a -> c p j a", p=P, j=4)
         wv_v = wv_bytes.rearrange("(c p j) n -> c p j n", p=P, j=4)
 
+        x_v = x.rearrange("(p i) d -> p i d", i=TILES)
+        z_v = z.rearrange("t (p i) d -> t p i d", i=TILES)
+        out_v = out.rearrange("(p i) d -> p i d", i=TILES)
+
         def load(name):
-            h = 1 if "B" in name else 0
-            cols = slice(h * HALF, (h + 1) * HALF)
             k = int(name[-1])
-            if name.startswith("x"):
-                nc.sync.dma_start(out=x_sb[k][:], in_=x[k * P : (k + 1) * P, :])
+            if name == "x0":
+                nc.sync.dma_start(out=x0[:], in_=x_v[:, 0, :])
+            elif name == "x12":
+                nc.sync.dma_start(out=x12[:], in_=x_v[:, 1:3, :])
+            elif name.startswith("zz"):
+                nc.sync.dma_start(out=z12[k][:], in_=z_v[k, :, 1:3, :])
             elif name.startswith("z"):
-                i = int(name[1])
-                nc.sync.dma_start(out=z_sb[i][k][:], in_=z[k, i * P : (i + 1) * P, :])
+                nc.sync.dma_start(out=z0[k][:], in_=z_v[k, :, 0, :])
             elif name.startswith("wq"):
-                for b in (2 * k, 2 * k + 1):
-                    nc.sync.dma_start(out=wq_sb[h][:, b, :, :], in_=wq_v[b, :, :, cols])
+                nc.sync.dma_start(out=wq_sb[k][:], in_=wq_v[k])
             elif name.startswith("wk"):
-                nc.sync.dma_start(out=wk_sb[h][k][:], in_=wk_v[k, :, :, cols])
+                nc.sync.dma_start(out=wk_sb[k][:], in_=wk_v[k])
             else:
                 nc.sync.dma_start(out=wv_sb[k][:], in_=wv_v[k])
 
-        nc.gpsimd.dma_start(out=wvs_sb[:], in_=wv_scale.rearrange("(c p j) o -> p c (j o)", p=P, j=4))
-        nc.gpsimd.dma_start(out=g_sb[:], in_=g.rearrange("(c p j) -> p c j", p=P, j=4))
-        for name in LOADS.split():
+        for n, name in enumerate(LOADS.split()):
+            if name.startswith("wv"):
+                first_wv = n
+                break
+        for n, name in enumerate(LOADS.split()):
+            if n == first_wv:
+                nc.sync.dma_start(out=wvs_sb[:], in_=wv_scale.rearrange("(c p j) o -> p c (j o)", p=P, j=4))
+                nc.sync.dma_start(out=g_sb[:], in_=g.rearrange("(c p j) -> p c j", p=P, j=4))
             load(name)
 
         wk_codes = [keep.tile([P, PASSES, HALF], U32, align_bytes=64, name=f"wkc{h}") for h in range(2)]
         wk_scales = [keep.tile([P, PASSES, HALF], U8, align_bytes=64, name=f"wks{h}") for h in range(2)]
         wv_codes = [keep.tile([P, D], U32, align_bytes=64, name=f"wvc{c}") for c in range(PASSES)]
         wv_scales = [keep.tile([P, D], U8, align_bytes=64, name=f"wvx{c}") for c in range(PASSES)]
-        xT_sb = [keep.tile([P, 4, P], F32, name=f"xT{i}") for i in range(TILES)]
+        xT_sb = [keep.tile([P, 4, 2, P], BF16, name=f"xT{i}") for i in range(TILES)]
         q_sb = [keep.tile([P, A], F32, name=f"q{i}") for i in range(TILES)]
         zq_codes = [[keep.tile([P, PASSES, P], U32, align_bytes=64, name=f"zc{i}_{t}") for t in range(T)] for i in range(TILES)]
         zq_scales = [[keep.tile([P, PASSES, P], U8, align_bytes=64, name=f"zs{i}_{t}") for t in range(T)] for i in range(TILES)]
@@ -118,7 +140,7 @@ def tile_adapterfusiontokenmixture_kernel(tc, x, z, wq, wk, wv_bytes, wv_scale, 
             return bank
 
 
-        wk_mid, banks, z_mid, neg, low, e_sb, total, parts, c_mid, wv_wide, wv_mid = ({} for _ in range(11))
+        z_perm, wk_mid, banks, z_mid, neg, low, e_sb, total, parts, c_mid, wv_wide, wv_mid = ({} for _ in range(12))
 
         def wk_tile(h, c):
             if (h, c) not in wk_mid:
@@ -135,8 +157,8 @@ def tile_adapterfusiontokenmixture_kernel(tc, x, z, wq, wk, wv_bytes, wv_scale, 
             if kind in ("wkiS", "wkiV", "wkq"):
                 h, c = "AB".index(rest[0]), int(rest[1])
                 mid = wk_tile(h, c)
-                src = wk_sb[h][c][:].rearrange("p j n -> p n j")
-                w = WK_SCALAR[h]
+                src = wk_sb[c][:, :, cols_of(h)].rearrange("p j n -> p n j")
+                w = WK_SCALAR[2 * h + c]
                 if kind == "wkiS":
                     nc.scalar.copy(out=mid[:, :w, :], in_=src[:, :w, :])
                 elif kind == "wkiV":
@@ -155,9 +177,11 @@ def tile_adapterfusiontokenmixture_kernel(tc, x, z, wq, wk, wv_bytes, wv_scale, 
                     if c not in wv_wide:
                         wide = keep.tile([P, 4, D], BF16, name=f"wvw{c}")
                         wv_wide[c] = wide
-                    nc.scalar.activation(
-                        out=wv_wide[c][:, j, :], in_=wv_sb[c][:, j, :].bitcast(FP8), func=ACT.Copy, scale=wvs_sb[:, c, j : j + 1]
-                    )
+                    src, scl = wv_sb[c][:, j, :].bitcast(FP8), wvs_sb[:, c, j : j + 1]
+                    if WD_ENGINE[4 * c + j] == "S":
+                        nc.scalar.activation(out=wv_wide[c][:, j, :], in_=src, func=ACT.Copy, scale=scl)
+                    else:
+                        nc.vector.tensor_scalar(out=wv_wide[c][:, j, :], in0=src, scalar1=scl, scalar2=None, op0=ALU.mult)
                 elif kind == "wvi":
                     s = int(rest[1])
                     if c not in wv_mid:
@@ -182,26 +206,28 @@ def tile_adapterfusiontokenmixture_kernel(tc, x, z, wq, wk, wv_bytes, wv_scale, 
             if kind == "xT":
                 bank = tp_bank()
                 banks["x", i] = bank
-                words = x_sb[i][:].bitcast(F32)
+                words = x_sb[i].bitcast(F32)
                 for b in range(4):
                     nc.tensor.transpose(bank[:, b, :], words[:, b * P : (b + 1) * P], ident[:])
             elif kind == "xTc":
-                nc.scalar.copy(out=xT_sb[i][:], in_=banks["x", i][:])
+                src = banks["x", i][:].rearrange("p b n -> p (b n)").bitcast(BF16).rearrange("p (b n e) -> p b e n", b=4, e=2)
+                if i == 1:
+                    nc.vector.tensor_copy(out=xT_sb[i][:], in_=src)
+                else:
+                    nc.scalar.copy(out=xT_sb[i][:], in_=src)
             elif kind == "q":
                 h, part = "AB".index(rest[1]), int(rest[2])
                 if part == 0:
                     acc = acc_bank()
                     banks["q", i, h] = acc
-                xT = xT_sb[i][:].rearrange("p b n -> p (b n)").bitcast(BF16)
-                for b in (2 * part, 2 * part + 1):
-                    for e in range(2):
-                        nc.tensor.matmul(
-                            out=banks["q", i, h][:],
-                            lhsT=xT[:, 2 * b * P + e : 2 * (b + 1) * P : 2],
-                            rhs=wq_sb[h][:, b, e, :],
-                            start=(b == 0 and e == 0),
-                            stop=(b == 3 and e == 1),
-                        )
+                for e in range(2):
+                    nc.tensor.matmul(
+                        out=banks["q", i, h][:],
+                        lhsT=xT_sb[i][:, part, e, :],
+                        rhs=wq_sb[part][:, e, cols_of(h)],
+                        start=(part == 0 and e == 0),
+                        stop=(part == 3 and e == 1),
+                    )
             elif kind == "qc":
                 h = "AB".index(rest[1])
                 nc.scalar.copy(out=q_sb[i][:, cols_of(h)], in_=banks["q", i, h][:])
@@ -209,13 +235,22 @@ def tile_adapterfusiontokenmixture_kernel(tc, x, z, wq, wk, wv_bytes, wv_scale, 
                 t = int(rest[1])
                 bank = tp_bank()
                 banks["z", i, t] = bank
-                words = z_sb[i][t][:].bitcast(F32)
+                words = z_sb[i][t].bitcast(F32)
                 for c in range(PASSES):
                     for u in range(2):
-                        nc.tensor.transpose(bank[:, 2 * c + u, :], words[:, 256 * c + u : 256 * (c + 1) : 2], ident[:])
+                        if ZP[4 * i + t] == "1":
+                            src = z_perm[i, t][:, c, u, :]
+                        else:
+                            src = words[:, 256 * c + u : 256 * (c + 1) : 2]
+                        nc.tensor.transpose(bank[:, 2 * c + u, :], src, ident[:])
+            elif kind == "zp":
+                t = int(rest[1])
+                perm = work.tile([P, PASSES, 2, P], F32, name="zperm", bufs=3)
+                z_perm[i, t] = perm
+                nc.scalar.copy(out=perm[:], in_=z_sb[i][t].bitcast(F32).rearrange("p (c n u) -> p c u n", c=PASSES, u=2))
             elif kind == "zTc":
                 t = int(rest[1])
-                mid = work.tile([P, PASSES, P, 2], F32, align_bytes=64, name="zmid", bufs=6)
+                mid = work.tile([P, PASSES, P, 2], F32, align_bytes=64, name="zmid", bufs=5)
                 z_mid[i, t] = mid
                 nc.scalar.copy(out=mid[:], in_=banks["z", i, t][:].rearrange("p (c u) n -> p c n u", u=2))
             elif kind == "zq":
@@ -280,7 +315,7 @@ def tile_adapterfusiontokenmixture_kernel(tc, x, z, wq, wk, wv_bytes, wv_scale, 
                     nc.vector.scalar_tensor_tensor(
                         out=part[:], in0=src, scalar=weight, in1=prev[:], op0=ALU.mult, op1=ALU.add
                     )
-                elif (MODES[i] == "D" and t in D_SCALAR) or MODES[i] in ("S2", "A") or (MODES[i] == "C" and t == 0):
+                elif (MODES[i][0] == "D" and str(t) in MODES[i]) or MODES[i] in ("S2", "A") or (MODES[i] == "C" and t == 0):
                     nc.scalar.activation(out=part[:], in_=src, func=ACT.Copy, scale=weight)
                 else:
                     nc.vector.tensor_scalar(out=part[:], in0=src, scalar1=weight, scalar2=None, op0=ALU.mult)
@@ -335,7 +370,7 @@ def tile_adapterfusiontokenmixture_kernel(tc, x, z, wq, wk, wv_bytes, wv_scale, 
                 h = "AB".index(rest[1])
                 res = work.tile([P, HALF], F32, name="res", bufs=3)
                 nc.vector.tensor_tensor(out=res[:], in0=banks["o", i, h][:], in1=x_sb[i][:, cols_of(h)], op=ALU.add)
-                nc.sync.dma_start(out=out[i * P : (i + 1) * P, cols_of(h)], in_=res[:])
+                nc.sync.dma_start(out=out_v[:, i, cols_of(h)], in_=res[:])
             else:
                 raise ValueError(op)
 

@@ -20,35 +20,38 @@ P = 128
 PASSES = 2
 HALF = 512
 TILES = N // P
-WK_SCALAR = (0, 0, 0, 512)
-WD_ENGINE = 'SSSSVSVV'
+WK_SCALAR = (512, 0, 0, 512)
+WD_ENGINE = 'SSVSSSSS'
 ZP = '000000000000'
-WARM = 6
-MODES = ('D012', 'D012', 'D012')
-LAST = {"D0": (0, 1, 2, 3), "D01": (0, 1, 2, 3), "D012": (0, 1, 2, 3), "S2": (1, 3), "C": (1, 3), "A": (3,)}
-WV_ENGINE = 'VSSSVSVV'
-PART_BUFS = {'pr2': 4, 'pr3': 4, 'pr0': 3, 'pr1': 3}
+WARM = 4
+FIN = 'GVV'
+LAST_FIN = 'fin2A'
+MODES = ('D012', 'D012', 'E01')
+LAST = {"E01": (0, 1, 3), "E0": (0, 1, 3), "D0": (0, 1, 2, 3), "D01": (0, 1, 2, 3), "D012": (0, 1, 2, 3), "S2": (1, 3), "C": (1, 3), "A": (3,)}
+WV_ENGINE = 'GGGGGGSG'
+PART_BUFS = {'pr1': 3, 'pr2': 3, 'pr3': 3, 'pr0': 3, 'ch3': 3}
 TP_BANKS, ACC_BANKS = 3, 5
-LOADS = "z00 x0 x12 wq0 zz0 z03 wq1 wv1 wq2 wk1 wq3 wk0 z02 z01 zz3 zz2 zz1 wv0"
+LOADS = "zz1 x12 zz0 x0 wq0 zz2 zz3 z00 z02 wq1 wk1 z03 z01 wq2 wk0 wq3 wv0 wv1"
 ORDER = (
-    "xT0 zT00 xTc0 zTc00 xT2 xT1 q0A0 q0B0 xTc2 q2B0 xTc1 q1A0 "
-    "zT20 zT03 zT10 q2A0 q2B1 zTc03 wd13 zTc10 q0B1 zTc20 zq10 wd10 "
-    "q0A1 q1A1 wd12 q2A1 wd11 q0B2 q2B2 q2A2 q1A2 q0A2 wvi13 wvi10 "
-    "wkiSB1 wkiVA1 q0A3 qc0A q1A3 zq20 qc1A wvi12 zq00 wkqA1 q0B3 qc0B "
-    "q2B3 q2A3 zT01 zT02 wkiVB0 zT23 zTc01 zT13 wkiVA0 zTc02 wkqB0 qc2B "
-    "wkqA0 zT12 zTc23 wkqB1 zq02 zTc12 qc2A zq01 k00A zq03 zTc13 wd01 "
-    "k00B k01B k03A k02A wd00 zT11 zq12 sc00A zT22 sc00B k03B sc03A "
-    "zq23 sc02A wvi11 sc01B zTc11 k02B sc03B wd03 k01A zq13 sc02B zTc22 "
-    "sc01A q1B0 zq11 k12A sadd0 smax0 exp0 wd02 k13A q1B1 q1B2 sc13A "
-    "q1B3 rec0 k10A qc1B k10B zq22 p0 k13B sc12A k11A pr012 wvi03 "
-    "pr013 k12B sc10A sc10B sc13B sc11A k11B wvi01 pr002 k22A zT21 sc12B "
-    "zTc21 pr000 sc11B pr003 sadd1 k20B sc22A smax1 exp1 wvi02 zq21 sc20B "
-    "k23B k23A k21A k22B pr011 rec1 sc23A sc23B p1 pr010 pr101 sc22B "
-    "k20A pr112 k21B cT01 pr001 pr100 sc21A sc21B sc20A pr103 sadd2 pr102 "
-    "pr113 smax2 cT00 exp2 pr110 pr111 cg01 rec2 cg00 cT10 cT11 p2 "
-    "pr211 wvq1 cg10 pr213 pr212 wvi00 pr203 pr200 pr210 wvq0 cT21 pr201 "
-    "cq0 cg11 pr202 cg21 cT20 cg20 cq1 cq2 cv0A cv0B cv2B fin0B "
-    "cv1B fin0A fin2B cv1A cv2A fin1B fin1A fin2A "
+    "zT11 zTc11 xT1 xTc1 zT20 zT10 zTc20 xT0 q1B0 q1A0 zTc10 xTc0 "
+    "zT12 zT22 zTc12 zT23 zTc22 zT00 zTc23 zT13 zq20 zTc00 zT02 zTc13 "
+    "xT2 zq13 q0B0 xTc2 q0B1 zq12 q0A0 q2A0 q2A1 q1A1 zq10 wkiVA1 "
+    "zT03 zTc02 wkiSB1 zq22 zT21 zq00 zT01 zq02 wkqA1 q0B2 q2A2 zTc01 "
+    "q1B1 q0A1 zq01 zTc03 q1A2 zq03 q0A2 wkiVB0 wkqB1 q1B2 zTc21 wkqB0 "
+    "q1B3 q0B3 zq11 q1A3 q0A3 wkiSA0 qc1B wkqA0 k00B zq23 wd02 zq21 "
+    "q2A3 qc1A qc0B qc0A k03B k00A qc2A sc00B sc03B sc00A wd01 wd03 "
+    "k10B k12A k01B wd10 k12B sc10B sc12A k01A k02A sc01B k11A wd11 "
+    "sc12B k03A k02B sc01A sc02A sc03A sc11A k11B k21A wd00 wd13 sc02B "
+    "k10A q2B0 wvi00 wvi01 sc21A wd12 sadd0 q2B1 sc11B k13A smax0 k13B "
+    "exp0 sc10A q2B2 rec0 sc13A p0 q2B3 wvi12 pr011 k23A qc2B pr002 "
+    "sc13B pr003 sadd1 pr013 sc23A wvi11 k23B pr000 smax1 k21B sc23B exp1 "
+    "sc21B k22A rec1 sc22A wvi10 pr001 k22B k20A p1 sc22B wvi02 k20B "
+    "sc20A pr012 sc20B pr010 pr103 cT00 pr101 sadd2 pr100 pr113 pr111 smax2 "
+    "pr102 exp2 cT01 pr112 cT10 wvi13 cg00 rec2 pr110 cg01 wvi03 p2 "
+    "cq00 cT11 pr202 cq01 wvq0 pr212 cv0B0 cg10 pr201 ch203 ch213 pr200 "
+    "pr211 pr210 cv0A0 cT20 wvq1 cT21 cg11 cv0A1 cq10 cv0B1 cg20 cv1A0 "
+    "cq11 cg21 cq20 fc0A fc0B cq21 fin0A cv1A1 cv1B0 fin1A cv1B1 cv2B0 "
+    "fin1B cv2B1 fin2B cv2A0 fin0B cv2A1 fin2A "
 )
 
 
@@ -72,7 +75,10 @@ def tile_adapterfusiontokenmixture_kernel(tc, x, z, wq, wk, wv_bytes, wv_scale, 
         z12 = [keep.tile([P, 2, D], BF16, name=f"z12_{t}") for t in range(T)]
         z_sb = [[z0[t][:] for t in range(T)], [z12[t][:, 0, :] for t in range(T)], [z12[t][:, 1, :] for t in range(T)]]
         wq_sb = [keep.tile([P, 2, A], BF16, name=f"wq{b}") for b in range(4)]
-        wk_sb = [keep.tile([P, 4, A], BF16, name=f"wk{c}") for c in range(PASSES)]
+        wk_sb = []
+        for c in range(PASSES):
+            raw = keep.tile([P, 4, A], BF16, name="raw", bufs=3)
+            wk_sb.append(raw)
         wv_sb = [keep.tile([P, 4, D], U8, name=f"wvb{c}") for c in range(PASSES)]
         wvs_sb = keep.tile([P, PASSES, 4], F32, name="wvs")
         g_sb = keep.tile([P, PASSES, 4], BF16, name="gsb")
@@ -175,7 +181,7 @@ def tile_adapterfusiontokenmixture_kernel(tc, x, z, wq, wk, wv_bytes, wv_scale, 
                 if kind == "wd":
                     j = int(rest[1])
                     if c not in wv_wide:
-                        wide = keep.tile([P, 4, D], BF16, name=f"wvw{c}")
+                        wide = keep.tile([P, 4, D], BF16, name="raw", bufs=3)
                         wv_wide[c] = wide
                     src, scl = wv_sb[c][:, j, :].bitcast(FP8), wvs_sb[:, c, j : j + 1]
                     if WD_ENGINE[4 * c + j] == "S":
@@ -245,12 +251,12 @@ def tile_adapterfusiontokenmixture_kernel(tc, x, z, wq, wk, wv_bytes, wv_scale, 
                         nc.tensor.transpose(bank[:, 2 * c + u, :], src, ident[:])
             elif kind == "zp":
                 t = int(rest[1])
-                perm = work.tile([P, PASSES, 2, P], F32, name="zperm", bufs=3)
+                perm = work.tile([P, PASSES, 2, P], F32, name="zperm", bufs=2)
                 z_perm[i, t] = perm
                 nc.scalar.copy(out=perm[:], in_=z_sb[i][t].bitcast(F32).rearrange("p (c n u) -> p c u n", c=PASSES, u=2))
             elif kind == "zTc":
                 t = int(rest[1])
-                mid = work.tile([P, PASSES, P, 2], F32, align_bytes=64, name="zmid", bufs=5)
+                mid = work.tile([P, PASSES, P, 2], F32, align_bytes=64, name="zmid", bufs=7)
                 z_mid[i, t] = mid
                 nc.scalar.copy(out=mid[:], in_=banks["z", i, t][:].rearrange("p (c u) n -> p c n u", u=2))
             elif kind == "zq":
@@ -315,7 +321,7 @@ def tile_adapterfusiontokenmixture_kernel(tc, x, z, wq, wk, wv_bytes, wv_scale, 
                     nc.vector.scalar_tensor_tensor(
                         out=part[:], in0=src, scalar=weight, in1=prev[:], op0=ALU.mult, op1=ALU.add
                     )
-                elif (MODES[i][0] == "D" and str(t) in MODES[i]) or MODES[i] in ("S2", "A") or (MODES[i] == "C" and t == 0):
+                elif (MODES[i][0] in "DE" and str(t) in MODES[i]) or MODES[i] in ("S2", "A") or (MODES[i][0] == "E" and t == 2):
                     nc.scalar.activation(out=part[:], in_=src, func=ACT.Copy, scale=weight)
                 else:
                     nc.vector.tensor_scalar(out=part[:], in0=src, scalar1=weight, scalar2=None, op0=ALU.mult)
@@ -347,30 +353,43 @@ def tile_adapterfusiontokenmixture_kernel(tc, x, z, wq, wk, wv_bytes, wv_scale, 
                     op=ALU.mult,
                 )
             elif kind == "cq":
+                c = int(rest[1])
                 nc.vector.quantize_mx(
-                    out=c_codes[i][:].rearrange("p c n -> p (c n)").bitcast(FP8X4),
-                    scales=c_scales[i][:].rearrange("p c n -> p (c n)"),
-                    in_=c_mid[i][:].rearrange("p c n j -> p (c n j)"),
+                    out=c_codes[i][:, c, :].bitcast(FP8X4),
+                    scales=c_scales[i][:, c, :],
+                    in_=c_mid[i][:, c, :, :].rearrange("p n j -> p (n j)"),
                 )
             elif kind == "cv":
                 h = "AB".index(rest[1])
-                acc = acc_bank()
-                banks["o", i, h] = acc
-                for c in range(PASSES):
-                    nc.tensor.matmul_mx(
-                        out=acc[:],
-                        lhsT=c_codes[i][:, c, :].bitcast(FP8X4),
-                        lhsT_scale=c_scales[i][:, c, :],
-                        rhs=wv_codes[c][:, cols_of(h)].bitcast(FP8X4),
-                        rhs_scale=wv_scales[c][:, cols_of(h)],
-                        start=(c == 0),
-                        stop=(c == PASSES - 1),
-                    )
+                c = int(rest[2])
+                if c == 0:
+                    acc = acc_bank()
+                    banks["o", i, h] = acc
+                nc.tensor.matmul_mx(
+                    out=banks["o", i, h][:],
+                    lhsT=c_codes[i][:, c, :].bitcast(FP8X4),
+                    lhsT_scale=c_scales[i][:, c, :],
+                    rhs=wv_codes[c][:, cols_of(h)].bitcast(FP8X4),
+                    rhs_scale=wv_scales[c][:, cols_of(h)],
+                    start=(c == 0),
+                    stop=(c == PASSES - 1),
+                )
+            elif kind == "fc":
+                h = "AB".index(rest[1])
+                flat = work.tile([P, HALF], F32, name="flat", bufs=2)
+                banks["f", i, h] = flat
+                nc.scalar.copy(out=flat[:], in_=banks["o", i, h][:])
             elif kind == "fin":
                 h = "AB".index(rest[1])
                 res = work.tile([P, HALF], F32, name="res", bufs=3)
-                nc.vector.tensor_tensor(out=res[:], in0=banks["o", i, h][:], in1=x_sb[i][:, cols_of(h)], op=ALU.add)
-                nc.sync.dma_start(out=out_v[:, i, cols_of(h)], in_=res[:])
+                if FIN[i] == "V":
+                    nc.vector.tensor_tensor(out=res[:], in0=banks["o", i, h][:], in1=x_sb[i][:, cols_of(h)], op=ALU.add)
+                else:
+                    nc.gpsimd.tensor_tensor(out=res[:], in0=banks["f", i, h][:], in1=x_sb[i][:, cols_of(h)], op=ALU.add)
+                if op == LAST_FIN:
+                    nc.scalar.dma_start(out=out_v[:, i, cols_of(h)], in_=res[:])
+                else:
+                    nc.sync.dma_start(out=out_v[:, i, cols_of(h)], in_=res[:])
             else:
                 raise ValueError(op)
 

@@ -20,38 +20,38 @@ P = 128
 PASSES = 2
 HALF = 512
 TILES = N // P
-WK_SCALAR = (512, 0, 0, 512)
-WD_ENGINE = 'SSVSSSSS'
+WK_SCALAR = (0, 0, 0, 256)
+WD_ENGINE = 'SVSVVSSS'
 ZP = '000000000000'
 WARM = 4
-FIN = 'GVV'
-LAST_FIN = 'fin2A'
-MODES = ('D012', 'D012', 'E01')
+FIN = 'VVV'
+LAST_FIN = 'fin2B'
+MODES = ('D012', 'E01', 'S2')
 LAST = {"E01": (0, 1, 3), "E0": (0, 1, 3), "D0": (0, 1, 2, 3), "D01": (0, 1, 2, 3), "D012": (0, 1, 2, 3), "S2": (1, 3), "C": (1, 3), "A": (3,)}
-WV_ENGINE = 'GGGGGGSG'
-PART_BUFS = {'pr1': 3, 'pr2': 3, 'pr3': 3, 'pr0': 3, 'ch3': 3}
+WV_ENGINE = 'SVSVSSSS'
+PART_BUFS = {'pr0': 3, 'pr1': 3, 'pr2': 3, 'pr3': 3, 'ch3': 3, 'ch1': 3}
 TP_BANKS, ACC_BANKS = 3, 5
-LOADS = "zz1 x12 zz0 x0 wq0 zz2 zz3 z00 z02 wq1 wk1 z03 z01 wq2 wk0 wq3 wv0 wv1"
+LOADS = "x0 x12 wq0 wv0 wq1 wq2 wk0 wq3 z00 z01 wk1 wv1 z02 z03 zz0 zz1 zz2 zz3"
 ORDER = (
-    "zT11 zTc11 xT1 xTc1 zT20 zT10 zTc20 xT0 q1B0 q1A0 zTc10 xTc0 "
-    "zT12 zT22 zTc12 zT23 zTc22 zT00 zTc23 zT13 zq20 zTc00 zT02 zTc13 "
-    "xT2 zq13 q0B0 xTc2 q0B1 zq12 q0A0 q2A0 q2A1 q1A1 zq10 wkiVA1 "
-    "zT03 zTc02 wkiSB1 zq22 zT21 zq00 zT01 zq02 wkqA1 q0B2 q2A2 zTc01 "
-    "q1B1 q0A1 zq01 zTc03 q1A2 zq03 q0A2 wkiVB0 wkqB1 q1B2 zTc21 wkqB0 "
-    "q1B3 q0B3 zq11 q1A3 q0A3 wkiSA0 qc1B wkqA0 k00B zq23 wd02 zq21 "
-    "q2A3 qc1A qc0B qc0A k03B k00A qc2A sc00B sc03B sc00A wd01 wd03 "
-    "k10B k12A k01B wd10 k12B sc10B sc12A k01A k02A sc01B k11A wd11 "
-    "sc12B k03A k02B sc01A sc02A sc03A sc11A k11B k21A wd00 wd13 sc02B "
-    "k10A q2B0 wvi00 wvi01 sc21A wd12 sadd0 q2B1 sc11B k13A smax0 k13B "
-    "exp0 sc10A q2B2 rec0 sc13A p0 q2B3 wvi12 pr011 k23A qc2B pr002 "
-    "sc13B pr003 sadd1 pr013 sc23A wvi11 k23B pr000 smax1 k21B sc23B exp1 "
-    "sc21B k22A rec1 sc22A wvi10 pr001 k22B k20A p1 sc22B wvi02 k20B "
-    "sc20A pr012 sc20B pr010 pr103 cT00 pr101 sadd2 pr100 pr113 pr111 smax2 "
-    "pr102 exp2 cT01 pr112 cT10 wvi13 cg00 rec2 pr110 cg01 wvi03 p2 "
-    "cq00 cT11 pr202 cq01 wvq0 pr212 cv0B0 cg10 pr201 ch203 ch213 pr200 "
-    "pr211 pr210 cv0A0 cT20 wvq1 cT21 cg11 cv0A1 cq10 cv0B1 cg20 cv1A0 "
-    "cq11 cg21 cq20 fc0A fc0B cq21 fin0A cv1A1 cv1B0 fin1A cv1B1 cv2B0 "
-    "fin1B cv2B1 fin2B cv2A0 fin0B cv2A1 fin2A "
+    "xT0 xTc0 xT1 xTc1 xT2 xTc2 q0B0 q0A0 q1A0 q2A0 wd00 wd01 "
+    "q0B1 wd02 wd03 q0A1 q1A1 q2A1 q0A2 q1A2 q2A2 wvi00 wvi01 wvi02 "
+    "wvi03 wkiVA0 q0A3 q1A3 q2A3 wkiVB0 wvq0 q0B2 wkqA0 wkqB0 wkiVA1 qc0A "
+    "q0B3 qc1A qc2A qc0B wkiSB1 wkiVB1 q1B0 q1B1 q1B2 q1B3 qc1B wkqA1 "
+    "zT00 zTc00 zT01 zTc01 zq00 zq01 wkqB1 wd10 zT02 zTc02 zT03 zTc03 "
+    "zq02 zq03 wd11 k00A k01A sc00A sc01A k00B k01B sc00B sc01B wd12 "
+    "k02A k03A sc02A sc03A wd13 zT10 zTc10 zT11 zTc11 wvi10 k02B k03B "
+    "sc02B sc03B zT12 zTc12 zT13 zTc13 zq10 zq11 sadd0 smax0 exp0 zq12 "
+    "zq13 wvi11 rec0 p0 k10A k11A sc10A sc11A k10B k11B sc10B sc11B "
+    "k12A k13A sc12A sc13A wvi12 k12B k13B sc12B sc13B wvi13 zT20 zTc20 "
+    "zT21 zTc21 pr000 pr001 pr002 pr003 zq20 zq21 sadd1 smax1 exp1 zT22 "
+    "zTc22 zT23 zTc23 q2B0 q2B1 q2B2 q2B3 qc2B wvq1 rec1 p1 zq22 "
+    "zq23 k20A k21A sc20A sc21A k20B k21B sc20B sc21B pr100 pr101 pr102 "
+    "ch103 pr010 pr011 pr012 pr013 cT00 cg00 k22A k23A sc22A sc23A k22B "
+    "k23B sc22B sc23B pr110 pr111 pr112 ch113 sadd2 smax2 exp2 cq00 cT01 "
+    "cg01 rec2 p2 cq01 cT10 cg10 cT11 cg11 cq10 cv0A0 cv0B0 pr200 "
+    "pr202 ch201 ch203 pr210 pr212 ch211 ch213 cv0A1 cv0B1 cq11 fin0A fin0B "
+    "cv1A0 cv1B0 cT20 cg20 cT21 cg21 cv1A1 cv1B1 cq20 cv2A0 cv2B0 cq21 "
+    "cv2A1 cv2B1 fin1A fin1B fin2A fin2B "
 )
 
 
@@ -256,7 +256,7 @@ def tile_adapterfusiontokenmixture_kernel(tc, x, z, wq, wk, wv_bytes, wv_scale, 
                 nc.scalar.copy(out=perm[:], in_=z_sb[i][t].bitcast(F32).rearrange("p (c n u) -> p c u n", c=PASSES, u=2))
             elif kind == "zTc":
                 t = int(rest[1])
-                mid = work.tile([P, PASSES, P, 2], F32, align_bytes=64, name="zmid", bufs=7)
+                mid = work.tile([P, PASSES, P, 2], F32, align_bytes=64, name="zmid", bufs=6)
                 z_mid[i, t] = mid
                 nc.scalar.copy(out=mid[:], in_=banks["z", i, t][:].rearrange("p (c u) n -> p c n u", u=2))
             elif kind == "zq":

from contextlib import ExitStack

import concourse.mybir as mybir
from concourse.masks import make_identity

N, T, D, A = 384, 4, 1024, 1024
FLOPS = 2 * N * D * A + 2 * T * N * D * A + 2 * N * D * D

F32 = mybir.dt.float32
BF16 = mybir.dt.bfloat16
U32 = mybir.dt.uint32
U8 = mybir.dt.uint8
FP8 = mybir.dt.float8_e4m3fn
FP8X4 = mybir.dt.float8_e4m3fn_x4
ALU = mybir.AluOpType
ACT = mybir.ActivationFunctionType
AX = mybir.AxisListType

P = 128
PASSES = 2
HALF = 512
TILES = N // P
WK_SCALAR = (0, 0, 0, 256)
WD_ENGINE = 'SVSVVSSS'
ZP = '000000000000'
WARM = 4
FIN = 'VVV'
LAST_FIN = 'fin2B'
MODES = ('D012', 'E01', 'S2')
LAST = {"E01": (0, 1, 3), "E0": (0, 1, 3), "D0": (0, 1, 2, 3), "D01": (0, 1, 2, 3), "D012": (0, 1, 2, 3), "S2": (1, 3), "C": (1, 3), "A": (3,)}
WV_ENGINE = 'SVSVSSSS'
PART_BUFS = {'pr0': 3, 'pr1': 3, 'pr2': 3, 'pr3': 3, 'ch3': 3, 'ch1': 3}
TP_BANKS, ACC_BANKS = 3, 5
LOADS = "x0 x12 wq0 wv0 wq1 wq2 wk0 wq3 z00 z01 wk1 wv1 z02 z03 zz0 zz1 zz2 zz3"
ORDER = (
    "xT0 xTc0 xT1 xTc1 xT2 xTc2 q0B0 q0A0 q1A0 q2A0 wd00 wd01 "
    "q0B1 wd02 wd03 q0A1 q1A1 q2A1 q0A2 q1A2 q2A2 wvi00 wvi01 wvi02 "
    "wvi03 wkiVA0 q0A3 q1A3 q2A3 wkiVB0 wvq0 q0B2 wkqA0 wkqB0 wkiVA1 qc0A "
    "q0B3 qc1A qc2A qc0B wkiSB1 wkiVB1 q1B0 q1B1 q1B2 q1B3 qc1B wkqA1 "
    "zT00 zTc00 zT01 zTc01 zq00 zq01 wkqB1 wd10 zT02 zTc02 zT03 zTc03 "
    "zq02 zq03 wd11 k00A k01A sc00A sc01A k00B k01B sc00B sc01B wd12 "
    "k02A k03A sc02A sc03A wd13 zT10 zTc10 zT11 zTc11 wvi10 k02B k03B "
    "sc02B sc03B zT12 zTc12 zT13 zTc13 zq10 zq11 sadd0 smax0 exp0 zq12 "
    "zq13 wvi11 rec0 p0 k10A k11A sc10A sc11A k10B k11B sc10B sc11B "
    "k12A k13A sc12A sc13A wvi12 k12B k13B sc12B sc13B wvi13 zT20 zTc20 "
    "zT21 zTc21 pr000 pr001 pr002 pr003 zq20 zq21 sadd1 smax1 exp1 zT22 "
    "zTc22 zT23 zTc23 q2B0 q2B1 q2B2 q2B3 qc2B wvq1 rec1 p1 zq22 "
    "zq23 k20A k21A sc20A sc21A k20B k21B sc20B sc21B pr100 pr101 pr102 "
    "ch103 pr010 pr011 pr012 pr013 cT00 cg00 k22A k23A sc22A sc23A k22B "
    "k23B sc22B sc23B pr110 pr111 pr112 ch113 sadd2 smax2 exp2 cq00 cT01 "
    "cg01 rec2 p2 cq01 cT10 cg10 cT11 cg11 cq10 cv0A0 cv0B0 pr200 "
    "pr202 ch201 ch203 pr210 pr212 ch211 ch213 cv0A1 cv0B1 cq11 fin0A fin0B "
    "cv1A0 cv1B0 cT20 cg20 cT21 cg21 cv1A1 cv1B1 cq20 cv2A0 cv2B0 cq21 "
    "cv2A1 cv2B1 fin1A fin1B fin2A fin2B "
)


def tile_adapterfusiontokenmixture_kernel(tc, x, z, wq, wk, wv_bytes, wv_scale, g, out):
    nc = tc.nc
    with ExitStack() as ctx:
        keep = ctx.enter_context(tc.tile_pool(name="keep", bufs=1))
        work = ctx.enter_context(tc.tile_pool(name="work", bufs=2))
        psum = ctx.enter_context(tc.psum_pool(name="psum", bufs=1))

        ident = keep.tile([P, P], F32, name="ident")
        make_identity(nc, ident[:])
        warm = keep.tile([P, 2], F32, name="warm")
        nc.vector.memset(warm[:], 0.0)
        nc.scalar.activation(out=warm[:, 1:2], in_=warm[:, 0:1], func=ACT.Exp)

        x0 = keep.tile([P, D], BF16, name="x0")
        x12 = keep.tile([P, 2, D], BF16, name="x12")
        x_sb = [x0[:], x12[:, 0, :], x12[:, 1, :]]
        z0 = [keep.tile([P, D], BF16, name=f"z0_{t}") for t in range(T)]
        z12 = [keep.tile([P, 2, D], BF16, name=f"z12_{t}") for t in range(T)]
        z_sb = [[z0[t][:] for t in range(T)], [z12[t][:, 0, :] for t in range(T)], [z12[t][:, 1, :] for t in range(T)]]
        wq_sb = [keep.tile([P, 2, A], BF16, name=f"wq{b}") for b in range(4)]
        wk_sb = []
        for c in range(PASSES):
            raw = keep.tile([P, 4, A], BF16, name="raw", bufs=3)
            wk_sb.append(raw)
        wv_sb = [keep.tile([P, 4, D], U8, name=f"wvb{c}") for c in range(PASSES)]
        wvs_sb = keep.tile([P, PASSES, 4], F32, name="wvs")
        g_sb = keep.tile([P, PASSES, 4], BF16, name="gsb")

        if WARM:
            zero = keep.tile([P, HALF], BF16, name="zero")
            nc.vector.memset(zero[:], 0.0)
            bank = psum.tile([P, HALF], F32, name="acc", tag="acc", bufs=5)
            for n in range(WARM):
                nc.tensor.matmul(out=bank[:], lhsT=zero[:, :P], rhs=zero[:], start=True, stop=True)
        wq_v = wq.rearrange("(b p e) a -> b p e a", p=P, e=2)
        wk_v = wk.rearrange("(c p j) a -> c p j a", p=P, j=4)
        wv_v = wv_bytes.rearrange("(c p j) n -> c p j n", p=P, j=4)

        x_v = x.rearrange("(p i) d -> p i d", i=TILES)
        z_v = z.rearrange("t (p i) d -> t p i d", i=TILES)
        out_v = out.rearrange("(p i) d -> p i d", i=TILES)

        def load(name):
            k = int(name[-1])
            if name == "x0":
                nc.sync.dma_start(out=x0[:], in_=x_v[:, 0, :])
            elif name == "x12":
                nc.sync.dma_start(out=x12[:], in_=x_v[:, 1:3, :])
            elif name.startswith("zz"):
                nc.sync.dma_start(out=z12[k][:], in_=z_v[k, :, 1:3, :])
            elif name.startswith("z"):
                nc.sync.dma_start(out=z0[k][:], in_=z_v[k, :, 0, :])
            elif name.startswith("wq"):
                nc.sync.dma_start(out=wq_sb[k][:], in_=wq_v[k])
            elif name.startswith("wk"):
                nc.sync.dma_start(out=wk_sb[k][:], in_=wk_v[k])
            else:
                nc.sync.dma_start(out=wv_sb[k][:], in_=wv_v[k])

        for n, name in enumerate(LOADS.split()):
            if name.startswith("wv"):
                first_wv = n
                break
        for n, name in enumerate(LOADS.split()):
            if n == first_wv:
                nc.sync.dma_start(out=wvs_sb[:], in_=wv_scale.rearrange("(c p j) o -> p c (j o)", p=P, j=4))
                nc.sync.dma_start(out=g_sb[:], in_=g.rearrange("(c p j) -> p c j", p=P, j=4))
            load(name)

        wk_codes = [keep.tile([P, PASSES, HALF], U32, align_bytes=64, name=f"wkc{h}") for h in range(2)]
        wk_scales = [keep.tile([P, PASSES, HALF], U8, align_bytes=64, name=f"wks{h}") for h in range(2)]
        wv_codes = [keep.tile([P, D], U32, align_bytes=64, name=f"wvc{c}") for c in range(PASSES)]
        wv_scales = [keep.tile([P, D], U8, align_bytes=64, name=f"wvx{c}") for c in range(PASSES)]
        xT_sb = [keep.tile([P, 4, 2, P], BF16, name=f"xT{i}") for i in range(TILES)]
        q_sb = [keep.tile([P, A], F32, name=f"q{i}") for i in range(TILES)]
        zq_codes = [[keep.tile([P, PASSES, P], U32, align_bytes=64, name=f"zc{i}_{t}") for t in range(T)] for i in range(TILES)]
        zq_scales = [[keep.tile([P, PASSES, P], U8, align_bytes=64, name=f"zs{i}_{t}") for t in range(T)] for i in range(TILES)]
        s_parts = [keep.tile([P, T, 2], F32, name=f"sp{i}") for i in range(TILES)]
        p_sb = [keep.tile([P, T], F32, name=f"p{i}") for i in range(TILES)]
        c_codes = [keep.tile([P, PASSES, P], U32, align_bytes=64, name=f"cc{i}") for i in range(TILES)]
        c_scales = [keep.tile([P, PASSES, P], U8, align_bytes=64, name=f"cs{i}") for i in range(TILES)]

        def tp_bank():
            bank = psum.tile([P, 4, P], F32, name="tp", tag="tp", bufs=TP_BANKS)
            return bank

        def acc_bank():
            bank = psum.tile([P, HALF], F32, name="acc", tag="acc", bufs=ACC_BANKS)
            return bank


        z_perm, wk_mid, banks, z_mid, neg, low, e_sb, total, parts, c_mid, wv_wide, wv_mid = ({} for _ in range(12))

        def wk_tile(h, c):
            if (h, c) not in wk_mid:
                mid = work.tile([P, HALF, 4], BF16, align_bytes=64, name="wkmid", bufs=4)
                wk_mid[h, c] = mid
            return wk_mid[h, c]

        def cols_of(h):
            return slice(h * HALF, (h + 1) * HALF)

        def do(op):
            kind = "".join(ch for ch in op if ch not in "0123456789AB")
            rest = op[len(kind):]
            if kind in ("wkiS", "wkiV", "wkq"):
                h, c = "AB".index(rest[0]), int(rest[1])
                mid = wk_tile(h, c)
                src = wk_sb[c][:, :, cols_of(h)].rearrange("p j n -> p n j")
                w = WK_SCALAR[2 * h + c]
                if kind == "wkiS":
                    nc.scalar.copy(out=mid[:, :w, :], in_=src[:, :w, :])
                elif kind == "wkiV":
                    nc.vector.tensor_copy(out=mid[:, w:, :], in_=src[:, w:, :])
                else:
                    nc.vector.quantize_mx(
                        out=wk_codes[h][:, c, :].bitcast(FP8X4),
                        scales=wk_scales[h][:, c, :],
                        in_=mid[:].rearrange("p n j -> p (n j)"),
                    )
                return
            if kind in ("wd", "wvi", "wvq"):
                c = int(rest[0])
                if kind == "wd":
                    j = int(rest[1])
                    if c not in wv_wide:
                        wide = keep.tile([P, 4, D], BF16, name="raw", bufs=3)
                        wv_wide[c] = wide
                    src, scl = wv_sb[c][:, j, :].bitcast(FP8), wvs_sb[:, c, j : j + 1]
                    if WD_ENGINE[4 * c + j] == "S":
                        nc.scalar.activation(out=wv_wide[c][:, j, :], in_=src, func=ACT.Copy, scale=scl)
                    else:
                        nc.vector.tensor_scalar(out=wv_wide[c][:, j, :], in0=src, scalar1=scl, scalar2=None, op0=ALU.mult)
                elif kind == "wvi":
                    s = int(rest[1])
                    if c not in wv_mid:
                        mid = keep.tile([P, D, 4], BF16, align_bytes=64, name=f"wvm{c}")
                        wv_mid[c] = mid
                    cols = slice(256 * s, 256 * (s + 1))
                    src = wv_wide[c][:, :, cols].rearrange("p j n -> p n j")
                    dst = wv_mid[c][:, cols, :]
                    eng = WV_ENGINE[4 * c + s]
                    if eng == "S":
                        nc.scalar.copy(out=dst, in_=src)
                    elif eng == "V":
                        nc.vector.tensor_copy(out=dst, in_=src)
                    else:
                        nc.gpsimd.tensor_scalar(out=dst, in0=src, scalar1=1.0, scalar2=0.0, op0=ALU.mult, op1=ALU.add)
                else:
                    nc.vector.quantize_mx(
                        out=wv_codes[c][:].bitcast(FP8X4), scales=wv_scales[c][:], in_=wv_mid[c][:].rearrange("p n j -> p (n j)")
                    )
                return
            i = int(rest[0])
            if kind == "xT":
                bank = tp_bank()
                banks["x", i] = bank
                words = x_sb[i].bitcast(F32)
                for b in range(4):
                    nc.tensor.transpose(bank[:, b, :], words[:, b * P : (b + 1) * P], ident[:])
            elif kind == "xTc":
                src = banks["x", i][:].rearrange("p b n -> p (b n)").bitcast(BF16).rearrange("p (b n e) -> p b e n", b=4, e=2)
                if i == 1:
                    nc.vector.tensor_copy(out=xT_sb[i][:], in_=src)
                else:
                    nc.scalar.copy(out=xT_sb[i][:], in_=src)
            elif kind == "q":
                h, part = "AB".index(rest[1]), int(rest[2])
                if part == 0:
                    acc = acc_bank()
                    banks["q", i, h] = acc
                for e in range(2):
                    nc.tensor.matmul(
                        out=banks["q", i, h][:],
                        lhsT=xT_sb[i][:, part, e, :],
                        rhs=wq_sb[part][:, e, cols_of(h)],
                        start=(part == 0 and e == 0),
                        stop=(part == 3 and e == 1),
                    )
            elif kind == "qc":
                h = "AB".index(rest[1])
                nc.scalar.copy(out=q_sb[i][:, cols_of(h)], in_=banks["q", i, h][:])
            elif kind == "zT":
                t = int(rest[1])
                bank = tp_bank()
                banks["z", i, t] = bank
                words = z_sb[i][t].bitcast(F32)
                for c in range(PASSES):
                    for u in range(2):
                        if ZP[4 * i + t] == "1":
                            src = z_perm[i, t][:, c, u, :]
                        else:
                            src = words[:, 256 * c + u : 256 * (c + 1) : 2]
                        nc.tensor.transpose(bank[:, 2 * c + u, :], src, ident[:])
            elif kind == "zp":
                t = int(rest[1])
                perm = work.tile([P, PASSES, 2, P], F32, name="zperm", bufs=2)
                z_perm[i, t] = perm
                nc.scalar.copy(out=perm[:], in_=z_sb[i][t].bitcast(F32).rearrange("p (c n u) -> p c u n", c=PASSES, u=2))
            elif kind == "zTc":
                t = int(rest[1])
                mid = work.tile([P, PASSES, P, 2], F32, align_bytes=64, name="zmid", bufs=6)
                z_mid[i, t] = mid
                nc.scalar.copy(out=mid[:], in_=banks["z", i, t][:].rearrange("p (c u) n -> p c n u", u=2))
            elif kind == "zq":
                t = int(rest[1])
                nc.vector.quantize_mx(
                    out=zq_codes[i][t][:].rearrange("p c n -> p (c n)").bitcast(FP8X4),
                    scales=zq_scales[i][t][:].rearrange("p c n -> p (c n)"),
                    in_=z_mid[i, t][:].rearrange("p c n u -> p (c n u)").bitcast(BF16),
                )
            elif kind == "k":
                t, h = int(rest[1]), "AB".index(rest[2])
                acc = acc_bank()
                banks["k", i, t, h] = acc
                for c in range(PASSES):
                    nc.tensor.matmul_mx(
                        out=acc[:],
                        lhsT=zq_codes[i][t][:, c, :].bitcast(FP8X4),
                        lhsT_scale=zq_scales[i][t][:, c, :],
                        rhs=wk_codes[h][:, c, :].bitcast(FP8X4),
                        rhs_scale=wk_scales[h][:, c, :],
                        start=(c == 0),
                        stop=(c == PASSES - 1),
                    )
            elif kind == "sc":
                t, h = int(rest[1]), "AB".index(rest[2])
                junk = work.tile([P, HALF], F32, name="junk", bufs=2)
                nc.vector.scalar_tensor_tensor(
                    out=junk[:],
                    in0=banks["k", i, t, h][:],
                    scalar=-1.0 / 32.0,
                    in1=q_sb[i][:, cols_of(h)],
                    op0=ALU.mult,
                    op1=ALU.mult,
                    accum_out=s_parts[i][:, t, h : h + 1],
                )
            elif kind == "sadd":
                tile = work.tile([P, T], F32, name="neg", bufs=3)
                neg[i] = tile
                nc.vector.tensor_reduce(out=tile[:], in_=s_parts[i][:], axis=AX.X, op=ALU.add)
            elif kind == "smax":
                tile = work.tile([P, 1], F32, name="low", bufs=3)
                low[i] = tile
                nc.vector.tensor_reduce(out=tile[:], in_=neg[i][:], axis=AX.X, op=ALU.min)
            elif kind == "exp":
                e = work.tile([P, T], F32, name="e", bufs=3)
                s = work.tile([P, 1], F32, name="total", bufs=3)
                e_sb[i], total[i] = e, s
                nc.scalar.activation(out=e[:], in_=neg[i][:], func=ACT.Exp, bias=low[i][:], scale=-1.0, accum_out=s[:])
            elif kind == "rec":
                inv = work.tile([P, 1], F32, name="inv", bufs=3)
                total[i, "inv"] = inv
                nc.vector.reciprocal(out=inv[:], in_=total[i][:])
            elif kind == "p":
                nc.vector.tensor_scalar(out=p_sb[i][:], in0=e_sb[i][:], scalar1=total[i, "inv"][:], scalar2=None, op0=ALU.mult)
            elif kind in ("pr", "ch"):
                c, t = int(rest[1]), int(rest[2])
                src = z_sb[i][t][:, 512 * c : 512 * (c + 1)].rearrange("p (n j) -> p j n", j=4)
                part = work.tile([P, 4, P], F32, name=f"{kind}{t}", bufs=PART_BUFS[kind + str(t)])
                weight = p_sb[i][:, t : t + 1]
                if kind == "ch":
                    prev = parts[i, c, t - 1]
                    nc.vector.scalar_tensor_tensor(
                        out=part[:], in0=src, scalar=weight, in1=prev[:], op0=ALU.mult, op1=ALU.add
                    )
                elif (MODES[i][0] in "DE" and str(t) in MODES[i]) or MODES[i] in ("S2", "A") or (MODES[i][0] == "E" and t == 2):
                    nc.scalar.activation(out=part[:], in_=src, func=ACT.Copy, scale=weight)
                else:
                    nc.vector.tensor_scalar(out=part[:], in0=src, scalar1=weight, scalar2=None, op0=ALU.mult)
                parts[i, c, t] = part
            elif kind == "cT":
                c = int(rest[1])
                bank = tp_bank()
                banks["c", i, c] = bank
                tiles = [parts[i, c, t] for t in LAST[MODES[i]]]
                for j in range(4):
                    for n in range(len(tiles)):
                        nc.tensor.matmul(
                            out=bank[:, j, :],
                            lhsT=tiles[n][:, j, :],
                            rhs=ident[:],
                            is_transpose=True,
                            start=(n == 0),
                            stop=(n == len(tiles) - 1),
                        )
            elif kind == "cg":
                c = int(rest[1])
                if i not in c_mid:
                    mid = work.tile([P, PASSES, P, 4], BF16, align_bytes=64, name="cmid", bufs=3)
                    c_mid[i] = mid
                nc.vector.tensor_tensor(
                    out=c_mid[i][:, c, :, :],
                    in0=banks["c", i, c][:].rearrange("p j n -> p n j"),
                    in1=g_sb[:, c, :].unsqueeze(1).to_broadcast([P, P, 4]),
                    op=ALU.mult,
                )
            elif kind == "cq":
                c = int(rest[1])
                nc.vector.quantize_mx(
                    out=c_codes[i][:, c, :].bitcast(FP8X4),
                    scales=c_scales[i][:, c, :],
                    in_=c_mid[i][:, c, :, :].rearrange("p n j -> p (n j)"),
                )
            elif kind == "cv":
                h = "AB".index(rest[1])
                c = int(rest[2])
                if c == 0:
                    acc = acc_bank()
                    banks["o", i, h] = acc
                nc.tensor.matmul_mx(
                    out=banks["o", i, h][:],
                    lhsT=c_codes[i][:, c, :].bitcast(FP8X4),
                    lhsT_scale=c_scales[i][:, c, :],
                    rhs=wv_codes[c][:, cols_of(h)].bitcast(FP8X4),
                    rhs_scale=wv_scales[c][:, cols_of(h)],
                    start=(c == 0),
                    stop=(c == PASSES - 1),
                )
            elif kind == "fc":
                h = "AB".index(rest[1])
                flat = work.tile([P, HALF], F32, name="flat", bufs=2)
                banks["f", i, h] = flat
                nc.scalar.copy(out=flat[:], in_=banks["o", i, h][:])
            elif kind == "fin":
                h = "AB".index(rest[1])
                res = work.tile([P, HALF], F32, name="res", bufs=3)
                if FIN[i] == "V":
                    nc.vector.tensor_tensor(out=res[:], in0=banks["o", i, h][:], in1=x_sb[i][:, cols_of(h)], op=ALU.add)
                else:
                    nc.gpsimd.tensor_tensor(out=res[:], in0=banks["f", i, h][:], in1=x_sb[i][:, cols_of(h)], op=ALU.add)
                if op == LAST_FIN:
                    nc.scalar.dma_start(out=out_v[:, i, cols_of(h)], in_=res[:])
                else:
                    nc.sync.dma_start(out=out_v[:, i, cols_of(h)], in_=res[:])
            else:
                raise ValueError(op)

        with tc.manual_schedule():
            for op in ORDER.split():
                do(op)
